import numpy as np
import ml_dtypes


def mxq(x, axis, fmt="e4m3"):
    dtype, down = {"e4m3": (ml_dtypes.float8_e4m3fn, 7), "e5m2": (ml_dtypes.float8_e5m2, 14)}[fmt]
    v = np.moveaxis(np.asarray(x, np.float32).astype(ml_dtypes.bfloat16).astype(np.float64), axis, -1)
    blocks = v.reshape(v.shape[:-1] + (-1, 32))
    amax = np.abs(blocks).max(-1, keepdims=True)
    byte = np.maximum(np.where(amax > 0, np.frexp(amax)[1] - 1 + 127, 0) - down, 1)
    scale = np.exp2(byte - 127.0)
    codes = (blocks / scale).astype(np.float32).astype(dtype).astype(np.float64)
    return np.moveaxis((codes * scale).reshape(v.shape), -1, axis)


WIDE = False


def mx_kscale(k):
    if not WIDE:
        return np.ones(k)
    levels = np.array([10, -10, 5, -5, 0])
    if k % 512:
        return np.exp2(np.random.permutation(np.resize(levels, k // 32))).repeat(32)
    a = np.empty((k // 512, 16))
    for p in range(k // 512):
        a[p, :8] = np.random.permutation(np.resize(levels, 8))
        for g in range(8):
            far = levels[np.abs(levels - a[p, g]) >= 10]
            a[p, g + 8] = far[np.random.randint(len(far))]
    return np.exp2(a.ravel()).repeat(32)


def f64(x):
    return np.asarray(x).astype(np.float64)


def striped(idx):
    return np.tile(idx.reshape(-1, 16).T, (8, 1)).astype(np.uint16)


def unstriped(offs):
    return offs[:16].T.reshape(-1).astype(np.int64)


def pack_weight(w):
    k, n = w.shape
    w = f64(np.asarray(w, np.float32).astype(ml_dtypes.bfloat16)).reshape(k // 32, 32, n)
    amax = np.abs(w).max(1)
    byte = np.clip(np.where(amax > 0, np.frexp(amax)[1] - 1 + 127 - 7, 1), 1, 254)
    scaled = (w * np.exp2(127.0 - byte)[:, None, :]).reshape(k, n).astype(np.float32)
    words = np.ascontiguousarray(scaled.reshape(k // 512, 128, 4, n).transpose(0, 1, 3, 2)).astype(ml_dtypes.float8_e4m3fn).view(np.uint8)
    return words, np.ascontiguousarray(byte.astype(np.uint8).reshape(k // 512, 16, n))


def unpack_weight(words, scales):
    g, p, n, _ = words.shape
    vals = np.ascontiguousarray(words).view(ml_dtypes.float8_e4m3fn).astype(np.float64) * np.repeat(np.exp2(scales.astype(np.float64) - 127.0), 8, axis=1)[..., None]
    return vals.transpose(0, 1, 3, 2).reshape(g * 512, n)


K, T, S, V = 512, 1024, 512, 512
P = 2 ** 7


def setup_inputs():
    n = np.random.standard_normal
    s = mx_kscale(K)[:, None]
    packed_xT = pack_weight(n((K, T)) * s)
    return {
        "x_words": packed_xT[0],
        "x_scales": packed_xT[1],
        "hT": (n((K, V)) / np.sqrt(K) / s).astype(np.float32),
        "norm": (np.tile(np.random.uniform(0.0, 1.0, T), (P, 1))).astype(np.float32),
        "post": (np.random.uniform(0.0, 1.0, (V, S))).astype(np.float32),
        "haz": (np.tile(np.random.uniform(0.01, 0.2, S), (P, 1))).astype(np.float32),
        "start": (np.tile((np.arange(S) == 0) * 1.0 + np.random.uniform(0.0, 0.001, S), (P, 1))).astype(np.float32),
        "offs": striped(np.random.permutation(T)[:S]),
    }


def reference(x_words, x_scales, hT, norm, post, haz, start, offs):
    hTq = mxq(f64(hT), 0, "e4m3")
    xq = unpack_weight(x_words, x_scales)[:, unstriped(offs)]
    y = (hTq.T @ xq) - (f64(norm)[:1][:, unstriped(offs)])
    jt = f64(post) * np.exp(0.7 * y)
    ch = jt * f64(haz)[:1]
    gr = jt - ch
    c0 = ch.sum(axis=1, keepdims=True)
    nw = np.pad(gr, ((0, 0), (1, 0)))[:, :S] + f64(start)[:1] * c0
    ev = nw.sum(axis=1, keepdims=True)
    return np.sqrt(100.0 * (nw / ev) + 0.01)

from contextlib import ExitStack

import concourse.mybir as mybir
from concourse.masks import make_identity

K, T, S, V = 512, 1024, 512, 512
FLOPS = 2 * K * S * V

F32 = mybir.dt.float32
BF16 = mybir.dt.bfloat16
I32 = mybir.dt.int32
U32 = mybir.dt.uint32
U16 = mybir.dt.uint16
U8 = mybir.dt.uint8
FP8X4 = mybir.dt.float8_e4m3fn_x4
ALU = mybir.AluOpType
ACT = mybir.ActivationFunctionType

P = 128
PACK = 4
BLOCKS = S // P
TILES = V // P
HALF = V // 2
NORM_ROWS = 32


def interleave(copy, grouped, raw):
    copy(
        out=grouped.rearrange("p (c i) r -> p c r i", i=4),
        in_=raw.rearrange("p r (c i) -> p c r i", i=4),
    )


def tile_picked_ybocpd_root_p_kernel(
    tc, x_words, x_scales, hT, norm, post, haz, start, offs, out
):
    nc = tc.nc
    with ExitStack() as ctx:
        keep = ctx.enter_context(tc.tile_pool(name="keep", bufs=1))
        psum = ctx.enter_context(tc.psum_pool(name="psum", bufs=1))
        ring = ctx.enter_context(tc.psum_pool(name="ring", bufs=3))

        offsets = keep.tile([P, S // 16], U16, name="offsets")
        word_table = keep.tile([P, T], I32, name="word_table", align_bytes=64)
        scale_table = keep.tile([P, T], U8, name="scale_table", align_bytes=64)
        norm_table = keep.tile([P, T], F32, name="norm_table", align_bytes=64)
        h_raw = [keep.tile([P, PACK, HALF], F32, name="h_raw%d" % u) for u in range(2)]
        haz_sb = keep.tile([P, S], F32, name="haz_sb")
        start_sb = keep.tile([P, S], F32, name="start_sb")
        post0 = keep.tile([P, S], F32, name="post0")
        post1 = keep.tile([P, S], F32, name="post1")
        post23 = keep.tile([P, 2, S], F32, name="post23")
        post_sb = [post0[:], post1[:], post23[:, 0, :], post23[:, 1, :]]
        shifted = keep.tile([P, TILES, S], F32, name="shifted")
        ident = keep.tile([P, P], F32, name="ident")

        nc.vector.memset(scale_table[:].bitcast(I32), 0)
        nc.vector.memset(norm_table[32:64, :], 0.0)
        nc.vector.memset(norm_table[64:128, :], 0.0)
        nc.vector.memset(shifted[:, :, 0:1], 0.0)
        make_identity(nc, ident[:])

        h_rows = hT.rearrange("(p r) t -> p r t", r=PACK)
        nc.sync.dma_start(offsets[:], offs)
        nc.sync.dma_start(norm_table[0:NORM_ROWS, :], norm[0:NORM_ROWS, :])
        nc.sync.dma_start(word_table[:], x_words[0].rearrange("p c r -> p (c r)").bitcast(I32))
        nc.sync.dma_start(h_raw[0][:], h_rows[:, :, 0:HALF])
        for q in range(4):
            nc.sync.dma_start(
                scale_table[32 * q : 32 * q + 4, :].bitcast(I32),
                x_scales[0, 4 * q : 4 * q + 4, :].bitcast(I32),
            )
        nc.sync.dma_start(h_raw[1][:], h_rows[:, :, HALF:V])
        nc.sync.dma_start(haz_sb[:], haz)
        nc.sync.dma_start(post0[:], post[0:P, :])
        nc.sync.dma_start(start_sb[:], start)
        nc.sync.dma_start(post1[:], post[P : 2 * P, :])
        nc.sync.dma_start(post23[:], post[2 * P : V, :].rearrange("(a p) j -> p a j", p=P))

        norm_picked = keep.tile([P, S], F32, name="norm_picked")
        nc.vector.tensor_copy(norm_picked[:], norm_table[:].indirect(offsets[:]))
        norm_turned = psum.tile([P, BLOCKS, P], F32, name="norm_turned")
        for b in range(BLOCKS):
            nc.tensor.transpose(norm_turned[:, b, :], norm_picked[:, b * P : (b + 1) * P], ident[:])
        exp_bias = keep.tile([P, BLOCKS], F32, name="exp_bias")
        nc.scalar.activation(out=exp_bias[:], in_=norm_turned[:, :, 0], func=ACT.Copy, scale=-0.7)

        groups = [(0, P), (P, P), (HALF, HALF)]
        grouped = [keep.tile([P, w, PACK], BF16, name="grouped%d" % g, align_bytes=64) for g, (t0, w) in enumerate(groups)]
        h_codes = [keep.tile([P, w], U32, name="h_codes%d" % g, align_bytes=64) for g, (t0, w) in enumerate(groups)]
        h_scales = [keep.tile([P, w], U8, name="h_scales%d" % g, align_bytes=64) for g, (t0, w) in enumerate(groups)]

        def quantise(g):
            nc.vector.quantize_mx(
                out=h_codes[g][:].bitcast(FP8X4),
                scales=h_scales[g][:],
                in_=grouped[g][:].rearrange("p w r -> p (w r)"),
            )

        interleave(nc.scalar.copy, grouped[0][:], h_raw[0][:, :, 0:P])
        interleave(nc.scalar.copy, grouped[1][:], h_raw[0][:, :, P:HALF])

        x_codes = [keep.tile([P, S // 2], U32, name="x_codes%d" % u, align_bytes=64) for u in range(2)]
        x_bytes = [keep.tile([P, S // 2], U8, name="x_bytes%d" % u, align_bytes=64) for u in range(2)]
        for u in range(2):
            nc.vector.tensor_copy(x_codes[u][:], word_table[:].bitcast(U32).indirect(offsets[:, 16 * u : 16 * (u + 1)]))
        nc.vector.tensor_copy(x_bytes[0][:], scale_table[:].indirect(offsets[:, 0:16]))
        quantise(0)
        nc.vector.tensor_copy(x_bytes[1][:], scale_table[:].indirect(offsets[:, 16:32]))
        quantise(1)
        interleave(nc.vector.tensor_copy, grouped[2][:], h_raw[1][:])
        quantise(2)

        for t in range(TILES):
            nc.gpsimd.tensor_scalar(
                out=post_sb[t][:, S - 1 : S], in0=post_sb[t][:, S - 1 : S],
                scalar1=haz_sb[:, S - 1 : S], scalar2=0.0, op0=ALU.mult, op1=ALU.add,
            )

        dens = []
        for g, (t0, w) in enumerate(groups):
            per_bank = S // w
            banks = [psum.tile([P, per_bank, w], F32, name="score%d_%d" % (g, i)) for i in range(BLOCKS // per_bank)]
            dens_turned = keep.tile([P, BLOCKS, w], F32, name="dens_turned%d" % g)
            for u in range(2):
                for b in (2 * u, 2 * u + 1):
                    cols = slice((b % 2) * P, (b % 2 + 1) * P)
                    nc.tensor.matmul_mx(
                        out=banks[b // per_bank][:, b % per_bank, :],
                        lhsT=x_codes[u][:, cols].bitcast(FP8X4),
                        lhsT_scale=x_bytes[u][:, cols],
                        rhs=h_codes[g][:].bitcast(FP8X4),
                        rhs_scale=h_scales[g][:],
                        start=True,
                        stop=True,
                    )
                for b in (2 * u, 2 * u + 1):
                    nc.scalar.activation(
                        out=dens_turned[:, b, :], in_=banks[b // per_bank][:, b % per_bank, :],
                        func=ACT.Exp, scale=0.7, bias=exp_bias[:, b : b + 1],
                    )
            for i in range(w // P):
                bank = ring.tile([P, S], F32, name="dens")
                for b in range(BLOCKS):
                    nc.tensor.transpose(bank[:, b * P : (b + 1) * P], dens_turned[:, b, i * P : (i + 1) * P], ident[:])
                dens.append(bank)

        start_copy = keep.tile([P, S], F32, name="start_copy")
        start_excess = keep.tile([P, 1], F32, name="start_excess")
        nc.scalar.activation(out=start_copy[:], in_=start_sb[:], func=ACT.Copy, bias=-1.0 / S, accum_out=start_excess[:])

        joint = [keep.tile([P, S], F32, name="joint%d" % t) for t in range(TILES)]
        mass = [keep.tile([P, S], F32, name="mass%d" % t) for t in range(TILES)]
        result = [keep.tile([P, S], F32, name="result%d" % t) for t in range(TILES)]
        stats = [keep.tile([P, 8], F32, name="stats%d" % t) for t in range(TILES)]
        root_scale = [keep.tile([P, 1], F32, name="root_scale%d" % t) for t in range(TILES)]

        def weigh(t):
            nc.vector.scalar_tensor_tensor(
                out=joint[t][:], in0=dens[t][:], scalar=1.0, in1=post_sb[t],
                op0=ALU.mult, op1=ALU.mult, accum_out=stats[t][:, 0:1],
            )

        def grow(t):
            nc.vector.scalar_tensor_tensor(
                out=shifted[:, t, 1:S], in0=haz_sb[:, 0 : S - 1], scalar=1.0, in1=joint[t][:, 0 : S - 1],
                op0=ALU.subtract, op1=ALU.mult, accum_out=stats[t][:, 1:2],
            )

        def change(t):
            nc.vector.tensor_tensor(out=stats[t][:, 2:3], in0=stats[t][:, 0:1], in1=stats[t][:, 1:2], op=ALU.add)

        def evidence(t):
            nc.vector.tensor_scalar(
                out=stats[t][:, 3:4], in0=stats[t][:, 2:3], scalar1=start_excess[:], scalar2=stats[t][:, 0:1],
                op0=ALU.mult, op1=ALU.add,
            )

        def invert(t):
            nc.vector.reciprocal(out=stats[t][:, 4:5], in_=stats[t][:, 3:4])
            nc.scalar.activation(out=root_scale[t][:], in_=stats[t][:, 4:5], func=ACT.Copy, scale=100.0)

        def finish(t, cols):
            nc.vector.scalar_tensor_tensor(
                out=mass[t][:, cols], in0=start_sb[:, cols], scalar=stats[t][:, 2:3], in1=shifted[:, t, cols],
                op0=ALU.mult, op1=ALU.subtract,
            )
            nc.scalar.activation(
                out=result[t][:, cols], in_=mass[t][:, cols], func=ACT.Sqrt, scale=root_scale[t][:], bias=0.01,
            )
            nc.sync.dma_start(out[t * P : (t + 1) * P, cols], result[t][:, cols])

        whole = slice(0, S)
        weigh(0)
        grow(0)
        for t in range(1, TILES):
            weigh(t)
            change(t - 1)
            grow(t)
            evidence(t - 1)
            if t == TILES - 1:
                change(t)
            invert(t - 1)
            if t == TILES - 1:
                evidence(t)
            finish(t - 1, whole)
        invert(TILES - 1)
        finish(TILES - 1, slice(0, S // 2))
        finish(TILES - 1, slice(S // 2, S))
